import numpy as np
import ml_dtypes


def mxq(x, axis, fmt="e4m3"):
    dtype, down = {"e4m3": (ml_dtypes.float8_e4m3fn, 7), "e5m2": (ml_dtypes.float8_e5m2, 14)}[fmt]
    v = np.moveaxis(np.asarray(x, np.float32).astype(ml_dtypes.bfloat16).astype(np.float64), axis, -1)
    blocks = v.reshape(v.shape[:-1] + (-1, 32))
    amax = np.abs(blocks).max(-1, keepdims=True)
    byte = np.maximum(np.where(amax > 0, np.frexp(amax)[1] - 1 + 127, 0) - down, 1)
    scale = np.exp2(byte - 127.0)
    codes = (blocks / scale).astype(np.float32).astype(dtype).astype(np.float64)
    return np.moveaxis((codes * scale).reshape(v.shape), -1, axis)


WIDE = False


def mx_kscale(k):
    if not WIDE:
        return np.ones(k)
    levels = np.array([10, -10, 5, -5, 0])
    if k % 512:
        return np.exp2(np.random.permutation(np.resize(levels, k // 32))).repeat(32)
    a = np.empty((k // 512, 16))
    for p in range(k // 512):
        a[p, :8] = np.random.permutation(np.resize(levels, 8))
        for g in range(8):
            far = levels[np.abs(levels - a[p, g]) >= 10]
            a[p, g + 8] = far[np.random.randint(len(far))]
    return np.exp2(a.ravel()).repeat(32)


def f64(x):
    return np.asarray(x).astype(np.float64)


def striped(idx):
    return np.tile(idx.reshape(-1, 16).T, (8, 1)).astype(np.uint16)


def unstriped(offs):
    return offs[:16].T.reshape(-1).astype(np.int64)


def striped8(idx):
    return np.concatenate([x.reshape(-1, 16).T for x in idx]).astype(np.uint16)


def runs(offs, k):
    lists = np.stack([offs[16 * r : 16 * r + 16].T.reshape(-1) for r in range(8)]).astype(np.int64)
    return lists[np.arange(k) % 512 // 64]


def pack_weight(w):
    k, n = w.shape
    w = f64(np.asarray(w, np.float32).astype(ml_dtypes.bfloat16)).reshape(k // 32, 32, n)
    amax = np.abs(w).max(1)
    byte = np.clip(np.where(amax > 0, np.frexp(amax)[1] - 1 + 127 - 7, 1), 1, 254)
    scaled = (w * np.exp2(127.0 - byte)[:, None, :]).reshape(k, n).astype(np.float32)
    words = np.ascontiguousarray(scaled.reshape(k // 512, 128, 4, n).transpose(0, 1, 3, 2)).astype(ml_dtypes.float8_e4m3fn).view(np.uint8)
    return words, np.ascontiguousarray(byte.astype(np.uint8).reshape(k // 512, 16, n))


def unpack_weight(words, scales):
    g, p, n, _ = words.shape
    vals = np.ascontiguousarray(words).view(ml_dtypes.float8_e4m3fn).astype(np.float64) * np.repeat(np.exp2(scales.astype(np.float64) - 127.0), 8, axis=1)[..., None]
    return vals.transpose(0, 1, 3, 2).reshape(g * 512, n)


K, T, S, V, N, H = 512, 2048, 512, 256, 512, 512


def setup_inputs():
    n = np.random.standard_normal
    s = mx_kscale(K)[:, None]
    u = mx_kscale(H)
    packed_xT = pack_weight(n((K, T)) * s)
    return {
        "x_words": packed_xT[0],
        "x_scales": packed_xT[1],
        "w1": (n((K, H)) / np.sqrt(K) / s).astype(np.float32),
        "gn": (np.random.uniform(0.5, 1.5, (H, 1)) * u[:, None]).astype(np.float32),
        "w2": (n((H, H)) / np.sqrt(H) / u[:, None]).astype(np.float32),
        "w3": (n((H, N)) / np.sqrt(H) / u[:, None]).astype(np.float32),
        "offs": striped(np.random.permutation(T)[:S]),
        "src": striped8(np.stack([np.random.permutation(S)[:V] for _ in range(8)])),
        "dst": striped8(np.stack([np.random.permutation(S)[:V] for _ in range(8)])),
    }


def reference(x_words, x_scales, w1, gn, w2, w3, offs, src, dst):
    xq = unpack_weight(x_words, x_scales)[:, unstriped(offs)]
    y = mxq(f64(w1), 0, "e4m3").T @ xq
    z = f64(gn) * y
    h = np.tanh(mxq(f64(w2), 0, "e4m3").T @ mxq(z, 0, "e4m3"))
    m1 = h[np.arange(H)[:, None], runs(src, H)]
    p = y.copy()
    p[np.arange(H)[:, None], runs(dst, H)] = m1
    z2 = f64(gn) * p
    return mxq(f64(w3), 0, "e4m3").T @ mxq(z2, 0, "e4m3")

@@ -1,0 +1,240 @@
+from contextlib import ExitStack
+
+import concourse.mybir as mybir
+
+K, T, S, V, N, H = 512, 2048, 512, 256, 512, 512
+FLOPS = 2 * K * H * S + 2 * H * H * S + 2 * H * N * S
+
+F32 = mybir.dt.float32
+BF16 = mybir.dt.bfloat16
+I32 = mybir.dt.int32
+U32 = mybir.dt.uint32
+U16 = mybir.dt.uint16
+U8 = mybir.dt.uint8
+FP8X4 = mybir.dt.float8_e4m3fn_x4
+MULT = mybir.AluOpType.mult
+COPY = mybir.ActivationFunctionType.Copy
+TANH = mybir.ActivationFunctionType.Tanh
+
+P = 128
+PACK = 4
+HALF = S // 2
+QUARTER = S // 4
+LIST_ROWS = 16
+
+
+def tile_picked_delivmat_none_p_kernel(tc, x_words, x_scales, w1, gn, w2, w3, offs, src, dst, out):
+    nc = tc.nc
+
+    with ExitStack() as ctx:
+        sb = ctx.enter_context(tc.tile_pool(name="sb", bufs=1))
+        psum = ctx.enter_context(tc.psum_pool(name="psum", bufs=1))
+
+        def tile(name, shape, dtype, tag=None):
+            return sb.tile(shape, dtype, name=name, tag=tag or name, align_bytes=64)
+
+        def bank(name, number, shape):
+            return psum.tile(shape, F32, name=name, tag="bank%d" % number)
+
+        def quantize(codes, scales, values):
+            nc.vector.quantize_mx(out=codes.bitcast(FP8X4), scales=scales, in_=values)
+
+        def product(acc, w_codes, w_scales, a_codes, a_scales):
+            nc.tensor.matmul_mx(out=acc, lhsT=w_codes.bitcast(FP8X4), lhsT_scale=w_scales,
+                                rhs=a_codes.bitcast(FP8X4), rhs_scale=a_scales, start=True, stop=True)
+
+        def load_half(name, w, h):
+            raw = tile("%s_raw%d" % (name, h), [P, PACK, HALF], F32)
+            nc.sync.dma_start(raw[:], w[:, h * HALF:(h + 1) * HALF].rearrange("(p j) c -> p j c", j=PACK))
+            return raw
+
+        def deal(copy, grouped, raw, h):
+            m = HALF // PACK
+            copy(grouped[:, :, h * m:(h + 1) * m, :].rearrange("p t m j -> p m j t"),
+                 raw[:].rearrange("p j (m t) -> p m j t", t=PACK))
+
+        zero = tile("zero", [P, 1], F32)
+        warm = tile("warm", [P, 1], F32)
+        nc.gpsimd.memset(zero[:], 0.0)
+        nc.scalar.activation(warm[:], zero[:], TANH)
+
+        xs_table = tile("xs_table", [P, T], U8)
+        nc.vector.memset(xs_table[:].bitcast(I32), 0)
+        w1_raw = [load_half("w1", w1, 0)]
+        offs_sb = sb.tile([P, S // LIST_ROWS], U16, name="offs_sb")
+        nc.sync.dma_start(offs_sb[:], offs)
+        for q in range(4):
+            nc.sync.dma_start(xs_table[32 * q:32 * q + 4, :].bitcast(I32), x_scales[0, 4 * q:4 * q + 4, :].bitcast(I32))
+        w1_raw.append(load_half("w1", w1, 1))
+        xw_table = tile("xw_table", [P, T], I32)
+        nc.sync.dma_start(xw_table[:], x_words[0].rearrange("p n r -> p (n r)").bitcast(I32))
+        gain = tile("gain", [P, PACK], F32)
+        nc.sync.dma_start(gain[:], gn.rearrange("(p t) o -> p (t o)", t=PACK))
+        w2_raw = [load_half("w2", w2, h) for h in range(2)]
+        src_sb = sb.tile([P, V // LIST_ROWS], U16, name="src_sb")
+        nc.sync.dma_start(src_sb[:], src)
+        dst_sb = sb.tile([P, V // LIST_ROWS], U16, name="dst_sb")
+        nc.sync.dma_start(dst_sb[:], dst)
+        w3_raw = [load_half("w3", w3, h) for h in range(2)]
+
+        w1_grouped = tile("w1_grouped", [P, PACK, P, PACK], BF16)
+        deal(nc.scalar.copy, w1_grouped, w1_raw[0], 0)
+        x_sc = tile("x_sc", [P, S], U8)
+        nc.vector.tensor_copy(x_sc[:], xs_table[:].indirect(offs_sb[:]))
+        deal(nc.vector.tensor_copy, w1_grouped, w1_raw[1], 1)
+        w1_codes = tile("w1_codes", [P, H], U32)
+        w1_sc = tile("w1_sc", [P, H], U8)
+        quantize(w1_codes[:], w1_sc[:], w1_grouped[:].rearrange("p t m j -> p (t m j)"))
+
+        gain_wide = tile("gain_wide", [P, PACK, V], F32)
+        nc.scalar.copy(gain_wide[:], gain[:].unsqueeze(2).to_broadcast([P, PACK, V]))
+
+        cols = HALF // LIST_ROWS
+        x_codes = []
+        for h in range(2):
+            picked = tile("x_codes%d" % h, [P, HALF], U32)
+            nc.vector.tensor_copy(picked[:], xw_table[:].bitcast(U32).indirect(offs_sb[:, h * cols:(h + 1) * cols]))
+            x_codes.append(picked)
+
+        w2_grouped = tile("w2_grouped", [P, PACK, P, PACK], BF16)
+        for h in range(2):
+            deal(nc.scalar.copy, w2_grouped, w2_raw[h], h)
+
+        y_banks = []
+        for c in range(4):
+            y = bank("y%d" % c, c, [P, PACK, QUARTER])
+            a = (c % 2) * QUARTER
+            for t in range(PACK):
+                product(y[:, t, :], w1_codes[:, t * P:(t + 1) * P], w1_sc[:, t * P:(t + 1) * P],
+                        x_codes[c // 2][:, a:a + QUARTER], x_sc[:, c * QUARTER:(c + 1) * QUARTER])
+            y_banks.append(y)
+        gain_x4 = gain[:].unsqueeze(1).to_broadcast([P, QUARTER, PACK])
+        z_codes, z_sc = [], []
+        z_grouped = [tile("z_grouped%d" % h, [P, HALF, PACK], BF16) for h in range(2)]
+        for h in range(2):
+            z_codes.append(tile("z_codes%d" % h, [P, HALF], U32))
+            z_sc.append(tile("z_sc%d" % h, [P, HALF], U8))
+
+        def make_z(c):
+            a = (c % 2) * QUARTER
+            nc.vector.tensor_tensor(z_grouped[c // 2][:, a:a + QUARTER, :], y_banks[c][:].rearrange("p t n -> p n t"), gain_x4, MULT)
+
+        def quantize_z(h):
+            quantize(z_codes[h][:], z_sc[h][:], z_grouped[h][:].rearrange("p n t -> p (n t)"))
+
+        order = (1, 3, 0, 2)
+        w2_codes = {}
+        w2_sc = [tile("w2_sc%d" % t, [P, P], U8) for t in range(PACK)]
+
+        def quantize_w2(t):
+            quantize(w2_codes[t], w2_sc[t][:], w2_grouped[:, t, :, :].rearrange("p m j -> p (m j)"))
+
+        make_z(0)
+        make_z(1)
+        make_z(2)
+        quantize_z(0)
+        make_z(3)
+        w2_first = tile("w2_first", [P, P], U32)
+        w2_codes.setdefault(order[0], w2_first[:])
+        quantize_w2(order[0])
+        quantize_z(1)
+        w2_later = tile("w2_later", [P, PACK - 1, P], U32, tag="z_grouped1")
+        for n, t in enumerate(order[1:]):
+            w2_codes.setdefault(t, w2_later[:, n, :])
+            quantize_w2(t)
+
+        windows = {}
+
+        def open_window(t, tag):
+            windows.setdefault(t, tile("window%d" % t, [P, S if t % 2 else 2 * S], F32, tag=tag))
+
+        def fill_window(t):
+            for c in range(4):
+                nc.scalar.activation(windows[t][:, c * QUARTER:(c + 1) * QUARTER], y_banks[c][:, t, :], COPY, scale=gain[:, t:t + 1])
+
+        a_banks = [[bank("a%d%d" % (pair, h), 4 + 2 * pair + h, [P, 2, HALF]) for h in range(2)] for pair in range(2)]
+        h_tiles = [tile("h%d" % t, [P, S], F32) for t in range(PACK)]
+
+        def messages(t):
+            for h in range(2):
+                product(a_banks[t // 2][h][:, t % 2, :], w2_codes[t], w2_sc[t][:], z_codes[h][:], z_sc[h][:])
+            for h in range(2):
+                nc.scalar.activation(h_tiles[t][:, h * HALF:(h + 1) * HALF], a_banks[t // 2][h][:, t % 2, :], TANH)
+
+        fetched = [tile("fetched%d" % t, [P, V], F32) for t in range(PACK)]
+
+        def gather(t):
+            nc.vector.tensor_copy(fetched[t][:], h_tiles[t][:].indirect(src_sb[:]))
+
+        def scatter(t):
+            nc.vector.tensor_tensor(windows[t][:].indirect(dst_sb[:]), fetched[t][:], gain_wide[:, t, :], MULT)
+            if t % 2:
+                nc.sync.dma_start(windows[t - 1][:, S:], windows[t][:])
+
+        w3_grouped = []
+
+        def group_w3(h):
+            grouped = tile("w3_grouped%d" % h, [P, HALF, PACK], BF16, tag="h%d" % order[h])
+            nc.scalar.copy(grouped[:].rearrange("p (c i) j -> p c j i", i=4),
+                           w3_raw[h][:].rearrange("p j (c i) -> p c j i", i=4))
+            w3_grouped.append(grouped)
+
+        z2_grouped = [tile("z2_grouped%d" % c, [P, QUARTER, 2, 2], BF16) for c in range(4)]
+
+        def weave(copy, pair, c):
+            both = windows[2 * pair][:].rearrange("p (e n) -> p n e", e=2)
+            copy(z2_grouped[c][:, :, pair, :], both[:, c * QUARTER:(c + 1) * QUARTER, :])
+
+        w3_codes = tile("w3_codes", [P, N], U32)
+        w3_sc = tile("w3_sc", [P, N], U8)
+
+        open_window(1, "w2_raw1")
+        fill_window(1)
+        messages(1)
+        messages(3)
+        gather(1)
+        gather(3)
+        messages(0)
+        open_window(0, "w2_sc0")
+        scatter(1)
+        open_window(3, "w2_sc3")
+        fill_window(3)
+        gather(0)
+        messages(2)
+        open_window(2, "w2_sc2")
+        scatter(3)
+        fill_window(0)
+        gather(2)
+        fill_window(2)
+        group_w3(0)
+        group_w3(1)
+        scatter(0)
+        for h in range(2):
+            quantize(w3_codes[:, h * HALF:(h + 1) * HALF], w3_sc[:, h * HALF:(h + 1) * HALF], w3_grouped[h][:].rearrange("p n j -> p (n j)"))
+        for c in range(4):
+            weave(nc.scalar.copy, 0, c)
+        scatter(2)
+
+        out_rows = out.rearrange("(u p) n -> p u n", p=P)
+        z2_codes = [tile("z2_codes%d" % c, [P, QUARTER], U32) for c in range(4)]
+        z2_sc = [tile("z2_sc%d" % c, [P, QUARTER], U8) for c in range(4)]
+
+        def quantize_z2(c):
+            quantize(z2_codes[c][:], z2_sc[c][:], z2_grouped[c][:].rearrange("p n a e -> p (n a e)"))
+
+        weave(nc.scalar.copy, 1, 3)
+        weave(nc.vector.tensor_copy, 1, 0)
+        weave(nc.vector.tensor_copy, 1, 1)
+        quantize_z2(0)
+        weave(nc.vector.tensor_copy, 1, 2)
+        for c in range(1, 4):
+            quantize_z2(c)
+        for c in range(4):
+            result = tile("result%d" % c, [P, 4, QUARTER], F32)
+            for pair in range(2):
+                o = bank("o%d%d" % (c, pair), 2 * c + pair, [P, 2, QUARTER])
+                for e in range(2):
+                    u = 2 * pair + e
+                    product(o[:, e, :], w3_codes[:, u * P:(u + 1) * P], w3_sc[:, u * P:(u + 1) * P], z2_codes[c][:], z2_sc[c][:])
+                (nc.scalar.copy if pair == 0 or c == 0 else nc.vector.tensor_copy)(result[:, 2 * pair:2 * pair + 2, :], o[:])
+            nc.sync.dma_start(out_rows[:, :, c * QUARTER:(c + 1) * QUARTER], result[:])

@@ -53,11 +53,6 @@ def tile_picked_delivmat_none_p_kernel(tc, x_words, x_scales, w1, gn, w2, w3, of
             copy(grouped[:, :, h * m:(h + 1) * m, :].rearrange("p t m j -> p m j t"),
                  raw[:].rearrange("p j (m t) -> p m j t", t=PACK))
 
-        zero = tile("zero", [P, 1], F32)
-        warm = tile("warm", [P, 1], F32)
-        nc.gpsimd.memset(zero[:], 0.0)
-        nc.scalar.activation(warm[:], zero[:], TANH)
-
         xs_table = tile("xs_table", [P, T], U8)
         nc.vector.memset(xs_table[:].bitcast(I32), 0)
         w1_raw = [load_half("w1", w1, 0)]
@@ -78,10 +73,10 @@ def tile_picked_delivmat_none_p_kernel(tc, x_words, x_scales, w1, gn, w2, w3, of
         w3_raw = [load_half("w3", w3, h) for h in range(2)]
 
         w1_grouped = tile("w1_grouped", [P, PACK, P, PACK], BF16)
-        deal(nc.scalar.copy, w1_grouped, w1_raw[0], 0)
+        deal(lambda to, of: nc.scalar.activation(to, of, COPY), w1_grouped, w1_raw[0], 0)
         x_sc = tile("x_sc", [P, S], U8)
         nc.vector.tensor_copy(x_sc[:], xs_table[:].indirect(offs_sb[:]))
-        deal(nc.vector.tensor_copy, w1_grouped, w1_raw[1], 1)
+        deal(nc.scalar.copy, w1_grouped, w1_raw[1], 1)
         w1_codes = tile("w1_codes", [P, H], U32)
         w1_sc = tile("w1_sc", [P, H], U8)
         quantize(w1_codes[:], w1_sc[:], w1_grouped[:].rearrange("p t m j -> p (t m j)"))
@@ -179,11 +174,13 @@ def tile_picked_delivmat_none_p_kernel(tc, x_words, x_scales, w1, gn, w2, w3, of
                            w3_raw[h][:].rearrange("p j (c i) -> p c j i", i=4))
             w3_grouped.append(grouped)
 
-        z2_grouped = [tile("z2_grouped%d" % c, [P, QUARTER, 2, 2], BF16) for c in range(4)]
+        z2_widths = (QUARTER, QUARTER, HALF)
+        z2_grouped = [tile("z2_grouped%d" % n, [P, width, 2, 2], BF16) for n, width in enumerate(z2_widths)]
 
         def weave(copy, pair, c):
             both = windows[2 * pair][:].rearrange("p (e n) -> p n e", e=2)
-            copy(z2_grouped[c][:, :, pair, :], both[:, c * QUARTER:(c + 1) * QUARTER, :])
+            a = max(c - 2, 0) * QUARTER
+            copy(z2_grouped[min(c, 2)][:, a:a + QUARTER, pair, :], both[:, c * QUARTER:(c + 1) * QUARTER, :])
 
         w3_codes = tile("w3_codes", [P, N], U32)
         w3_sc = tile("w3_sc", [P, N], U8)
@@ -216,25 +213,30 @@ def tile_picked_delivmat_none_p_kernel(tc, x_words, x_scales, w1, gn, w2, w3, of
         scatter(2)
 
         out_rows = out.rearrange("(u p) n -> p u n", p=P)
-        z2_codes = [tile("z2_codes%d" % c, [P, QUARTER], U32) for c in range(4)]
-        z2_sc = [tile("z2_sc%d" % c, [P, QUARTER], U8) for c in range(4)]
+        z2_codes = [tile("z2_codes%d" % n, [P, width], U32) for n, width in enumerate(z2_widths)]
+        z2_sc = [tile("z2_sc%d" % n, [P, width], U8) for n, width in enumerate(z2_widths)]
 
-        def quantize_z2(c):
-            quantize(z2_codes[c][:], z2_sc[c][:], z2_grouped[c][:].rearrange("p n a e -> p (n a e)"))
+        def quantize_z2(n):
+            quantize(z2_codes[n][:], z2_sc[n][:], z2_grouped[n][:].rearrange("p n a e -> p (n a e)"))
 
         weave(nc.scalar.copy, 1, 3)
         weave(nc.vector.tensor_copy, 1, 0)
         weave(nc.vector.tensor_copy, 1, 1)
         quantize_z2(0)
         weave(nc.vector.tensor_copy, 1, 2)
-        for c in range(1, 4):
-            quantize_z2(c)
-        for c in range(4):
-            result = tile("result%d" % c, [P, 4, QUARTER], F32)
-            for pair in range(2):
-                o = bank("o%d%d" % (c, pair), 2 * c + pair, [P, 2, QUARTER])
-                for e in range(2):
-                    u = 2 * pair + e
-                    product(o[:, e, :], w3_codes[:, u * P:(u + 1) * P], w3_sc[:, u * P:(u + 1) * P], z2_codes[c][:], z2_sc[c][:])
-                (nc.scalar.copy if pair == 0 or c == 0 else nc.vector.tensor_copy)(result[:, 2 * pair:2 * pair + 2, :], o[:])
-            nc.sync.dma_start(out_rows[:, :, c * QUARTER:(c + 1) * QUARTER], result[:])
+        quantize_z2(1)
+        quantize_z2(2)
+        number = 0
+        for n, u0, rows in ((0, 0, 2), (0, 2, 2), (1, 0, 4), (2, 0, 2), (2, 2, 2)):
+            width = z2_widths[n]
+            first = n * QUARTER
+            per_bank = HALF // width
+            result = tile("result%d" % number, [P, rows, width], F32)
+            for r0 in range(0, rows, per_bank):
+                o = bank("o%d" % number, number, [P, per_bank, width])
+                for e in range(per_bank):
+                    u = u0 + r0 + e
+                    product(o[:, e, :], w3_codes[:, u * P:(u + 1) * P], w3_sc[:, u * P:(u + 1) * P], z2_codes[n][:], z2_sc[n][:])
+                (nc.scalar.copy if number % 2 == 0 or number == 1 else nc.vector.tensor_copy)(result[:, r0:r0 + per_bank, :], o[:])
+                number = number + 1
+            nc.sync.dma_start(out_rows[:, u0:u0 + rows, first:first + width], result[:])

from contextlib import ExitStack

import concourse.mybir as mybir

K, T, S, V, N, H = 512, 2048, 512, 256, 512, 512
FLOPS = 2 * K * H * S + 2 * H * H * S + 2 * H * N * S

F32 = mybir.dt.float32
BF16 = mybir.dt.bfloat16
I32 = mybir.dt.int32
U32 = mybir.dt.uint32
U16 = mybir.dt.uint16
U8 = mybir.dt.uint8
FP8X4 = mybir.dt.float8_e4m3fn_x4
MULT = mybir.AluOpType.mult
COPY = mybir.ActivationFunctionType.Copy
TANH = mybir.ActivationFunctionType.Tanh

P = 128
PACK = 4
HALF = S // 2
QUARTER = S // 4
LIST_ROWS = 16


def tile_picked_delivmat_none_p_kernel(tc, x_words, x_scales, w1, gn, w2, w3, offs, src, dst, out):
    nc = tc.nc

    with ExitStack() as ctx:
        sb = ctx.enter_context(tc.tile_pool(name="sb", bufs=1))
        psum = ctx.enter_context(tc.psum_pool(name="psum", bufs=1))

        def tile(name, shape, dtype, tag=None):
            return sb.tile(shape, dtype, name=name, tag=tag or name, align_bytes=64)

        def bank(name, number, shape):
            return psum.tile(shape, F32, name=name, tag="bank%d" % number)

        def quantize(codes, scales, values):
            nc.vector.quantize_mx(out=codes.bitcast(FP8X4), scales=scales, in_=values)

        def product(acc, w_codes, w_scales, a_codes, a_scales):
            nc.tensor.matmul_mx(out=acc, lhsT=w_codes.bitcast(FP8X4), lhsT_scale=w_scales,
                                rhs=a_codes.bitcast(FP8X4), rhs_scale=a_scales, start=True, stop=True)

        def load_half(name, w, h):
            raw = tile("%s_raw%d" % (name, h), [P, PACK, HALF], F32)
            nc.sync.dma_start(raw[:], w[:, h * HALF:(h + 1) * HALF].rearrange("(p j) c -> p j c", j=PACK))
            return raw

        def deal(copy, grouped, raw, h):
            m = HALF // PACK
            copy(grouped[:, :, h * m:(h + 1) * m, :].rearrange("p t m j -> p m j t"),
                 raw[:].rearrange("p j (m t) -> p m j t", t=PACK))

        xs_table = tile("xs_table", [P, T], U8)
        nc.vector.memset(xs_table[:].bitcast(I32), 0)
        w1_raw = [load_half("w1", w1, 0)]
        offs_sb = sb.tile([P, S // LIST_ROWS], U16, name="offs_sb")
        nc.sync.dma_start(offs_sb[:], offs)
        for q in range(4):
            nc.sync.dma_start(xs_table[32 * q:32 * q + 4, :].bitcast(I32), x_scales[0, 4 * q:4 * q + 4, :].bitcast(I32))
        w1_raw.append(load_half("w1", w1, 1))
        xw_table = tile("xw_table", [P, T], I32)
        nc.sync.dma_start(xw_table[:], x_words[0].rearrange("p n r -> p (n r)").bitcast(I32))
        gain = tile("gain", [P, PACK], F32)
        nc.sync.dma_start(gain[:], gn.rearrange("(p t) o -> p (t o)", t=PACK))
        w2_raw = [load_half("w2", w2, h) for h in range(2)]
        src_sb = sb.tile([P, V // LIST_ROWS], U16, name="src_sb")
        nc.sync.dma_start(src_sb[:], src)
        dst_sb = sb.tile([P, V // LIST_ROWS], U16, name="dst_sb")
        nc.sync.dma_start(dst_sb[:], dst)
        w3_raw = [load_half("w3", w3, h) for h in range(2)]

        w1_grouped = tile("w1_grouped", [P, PACK, P, PACK], BF16)
        deal(lambda to, of: nc.scalar.activation(to, of, COPY), w1_grouped, w1_raw[0], 0)
        x_sc = tile("x_sc", [P, S], U8)
        nc.vector.tensor_copy(x_sc[:], xs_table[:].indirect(offs_sb[:]))
        deal(nc.scalar.copy, w1_grouped, w1_raw[1], 1)
        w1_codes = tile("w1_codes", [P, H], U32)
        w1_sc = tile("w1_sc", [P, H], U8)
        quantize(w1_codes[:], w1_sc[:], w1_grouped[:].rearrange("p t m j -> p (t m j)"))

        gain_wide = tile("gain_wide", [P, PACK, V], F32)
        nc.scalar.copy(gain_wide[:], gain[:].unsqueeze(2).to_broadcast([P, PACK, V]))

        cols = HALF // LIST_ROWS
        x_codes = []
        for h in range(2):
            picked = tile("x_codes%d" % h, [P, HALF], U32)
            nc.vector.tensor_copy(picked[:], xw_table[:].bitcast(U32).indirect(offs_sb[:, h * cols:(h + 1) * cols]))
            x_codes.append(picked)

        w2_grouped = tile("w2_grouped", [P, PACK, P, PACK], BF16)
        for h in range(2):
            deal(nc.scalar.copy, w2_grouped, w2_raw[h], h)

        y_banks = []
        for c in range(4):
            y = bank("y%d" % c, c, [P, PACK, QUARTER])
            a = (c % 2) * QUARTER
            for t in range(PACK):
                product(y[:, t, :], w1_codes[:, t * P:(t + 1) * P], w1_sc[:, t * P:(t + 1) * P],
                        x_codes[c // 2][:, a:a + QUARTER], x_sc[:, c * QUARTER:(c + 1) * QUARTER])
            y_banks.append(y)
        gain_x4 = gain[:].unsqueeze(1).to_broadcast([P, QUARTER, PACK])
        z_codes, z_sc = [], []
        z_grouped = [tile("z_grouped%d" % h, [P, HALF, PACK], BF16) for h in range(2)]
        for h in range(2):
            z_codes.append(tile("z_codes%d" % h, [P, HALF], U32))
            z_sc.append(tile("z_sc%d" % h, [P, HALF], U8))

        def make_z(c):
            a = (c % 2) * QUARTER
            nc.vector.tensor_tensor(z_grouped[c // 2][:, a:a + QUARTER, :], y_banks[c][:].rearrange("p t n -> p n t"), gain_x4, MULT)

        def quantize_z(h):
            quantize(z_codes[h][:], z_sc[h][:], z_grouped[h][:].rearrange("p n t -> p (n t)"))

        order = (1, 3, 0, 2)
        w2_codes = {}
        w2_sc = [tile("w2_sc%d" % t, [P, P], U8) for t in range(PACK)]

        def quantize_w2(t):
            quantize(w2_codes[t], w2_sc[t][:], w2_grouped[:, t, :, :].rearrange("p m j -> p (m j)"))

        make_z(0)
        make_z(1)
        make_z(2)
        quantize_z(0)
        make_z(3)
        w2_first = tile("w2_first", [P, P], U32)
        w2_codes.setdefault(order[0], w2_first[:])
        quantize_w2(order[0])
        quantize_z(1)
        w2_later = tile("w2_later", [P, PACK - 1, P], U32, tag="z_grouped1")
        for n, t in enumerate(order[1:]):
            w2_codes.setdefault(t, w2_later[:, n, :])
            quantize_w2(t)

        windows = {}

        def open_window(t, tag):
            windows.setdefault(t, tile("window%d" % t, [P, S if t % 2 else 2 * S], F32, tag=tag))

        def fill_window(t):
            for c in range(4):
                nc.scalar.activation(windows[t][:, c * QUARTER:(c + 1) * QUARTER], y_banks[c][:, t, :], COPY, scale=gain[:, t:t + 1])

        a_banks = [[bank("a%d%d" % (pair, h), 4 + 2 * pair + h, [P, 2, HALF]) for h in range(2)] for pair in range(2)]
        h_tiles = [tile("h%d" % t, [P, S], F32) for t in range(PACK)]

        def messages(t):
            for h in range(2):
                product(a_banks[t // 2][h][:, t % 2, :], w2_codes[t], w2_sc[t][:], z_codes[h][:], z_sc[h][:])
            for h in range(2):
                nc.scalar.activation(h_tiles[t][:, h * HALF:(h + 1) * HALF], a_banks[t // 2][h][:, t % 2, :], TANH)

        fetched = [tile("fetched%d" % t, [P, V], F32) for t in range(PACK)]

        def gather(t):
            nc.vector.tensor_copy(fetched[t][:], h_tiles[t][:].indirect(src_sb[:]))

        def scatter(t):
            nc.vector.tensor_tensor(windows[t][:].indirect(dst_sb[:]), fetched[t][:], gain_wide[:, t, :], MULT)
            if t % 2:
                nc.sync.dma_start(windows[t - 1][:, S:], windows[t][:])

        w3_grouped = []

        def group_w3(h):
            grouped = tile("w3_grouped%d" % h, [P, HALF, PACK], BF16, tag="h%d" % order[h])
            nc.scalar.copy(grouped[:].rearrange("p (c i) j -> p c j i", i=4),
                           w3_raw[h][:].rearrange("p j (c i) -> p c j i", i=4))
            w3_grouped.append(grouped)

        z2_widths = (QUARTER, QUARTER, HALF)
        z2_grouped = [tile("z2_grouped%d" % n, [P, width, 2, 2], BF16) for n, width in enumerate(z2_widths)]

        def weave(copy, pair, c):
            both = windows[2 * pair][:].rearrange("p (e n) -> p n e", e=2)
            a = max(c - 2, 0) * QUARTER
            copy(z2_grouped[min(c, 2)][:, a:a + QUARTER, pair, :], both[:, c * QUARTER:(c + 1) * QUARTER, :])

        w3_codes = tile("w3_codes", [P, N], U32)
        w3_sc = tile("w3_sc", [P, N], U8)

        open_window(1, "w2_raw1")
        fill_window(1)
        messages(1)
        messages(3)
        gather(1)
        gather(3)
        messages(0)
        open_window(0, "w2_sc0")
        scatter(1)
        open_window(3, "w2_sc3")
        fill_window(3)
        gather(0)
        messages(2)
        open_window(2, "w2_sc2")
        scatter(3)
        fill_window(0)
        gather(2)
        fill_window(2)
        group_w3(0)
        group_w3(1)
        scatter(0)
        for h in range(2):
            quantize(w3_codes[:, h * HALF:(h + 1) * HALF], w3_sc[:, h * HALF:(h + 1) * HALF], w3_grouped[h][:].rearrange("p n j -> p (n j)"))
        for c in range(4):
            weave(nc.scalar.copy, 0, c)
        scatter(2)

        out_rows = out.rearrange("(u p) n -> p u n", p=P)
        z2_codes = [tile("z2_codes%d" % n, [P, width], U32) for n, width in enumerate(z2_widths)]
        z2_sc = [tile("z2_sc%d" % n, [P, width], U8) for n, width in enumerate(z2_widths)]

        def quantize_z2(n):
            quantize(z2_codes[n][:], z2_sc[n][:], z2_grouped[n][:].rearrange("p n a e -> p (n a e)"))

        weave(nc.scalar.copy, 1, 3)
        weave(nc.vector.tensor_copy, 1, 0)
        weave(nc.vector.tensor_copy, 1, 1)
        quantize_z2(0)
        weave(nc.vector.tensor_copy, 1, 2)
        quantize_z2(1)
        quantize_z2(2)
        number = 0
        for n, u0, rows in ((0, 0, 2), (0, 2, 2), (1, 0, 4), (2, 0, 2), (2, 2, 2)):
            width = z2_widths[n]
            first = n * QUARTER
            per_bank = HALF // width
            result = tile("result%d" % number, [P, rows, width], F32)
            for r0 in range(0, rows, per_bank):
                o = bank("o%d" % number, number, [P, per_bank, width])
                for e in range(per_bank):
                    u = u0 + r0 + e
                    product(o[:, e, :], w3_codes[:, u * P:(u + 1) * P], w3_sc[:, u * P:(u + 1) * P], z2_codes[n][:], z2_sc[n][:])
                (nc.scalar.copy if number % 2 == 0 or number == 1 else nc.vector.tensor_copy)(result[:, r0:r0 + per_bank, :], o[:])
                number = number + 1
            nc.sync.dma_start(out_rows[:, u0:u0 + rows, first:first + width], result[:])
